import numpy as np
import ml_dtypes


def mxq(x, axis, fmt="e4m3"):
    dtype, down = {"e4m3": (ml_dtypes.float8_e4m3fn, 7), "e5m2": (ml_dtypes.float8_e5m2, 14)}[fmt]
    v = np.moveaxis(np.asarray(x, np.float32).astype(ml_dtypes.bfloat16).astype(np.float64), axis, -1)
    blocks = v.reshape(v.shape[:-1] + (-1, 32))
    amax = np.abs(blocks).max(-1, keepdims=True)
    byte = np.maximum(np.where(amax > 0, np.frexp(amax)[1] - 1 + 127, 0) - down, 1)
    scale = np.exp2(byte - 127.0)
    codes = (blocks / scale).astype(np.float32).astype(dtype).astype(np.float64)
    return np.moveaxis((codes * scale).reshape(v.shape), -1, axis)


WIDE = False


def mx_kscale(k):
    if not WIDE:
        return np.ones(k)
    levels = np.array([10, -10, 5, -5, 0])
    if k % 512:
        return np.exp2(np.random.permutation(np.resize(levels, k // 32))).repeat(32)
    a = np.empty((k // 512, 16))
    for p in range(k // 512):
        a[p, :8] = np.random.permutation(np.resize(levels, 8))
        for g in range(8):
            far = levels[np.abs(levels - a[p, g]) >= 10]
            a[p, g + 8] = far[np.random.randint(len(far))]
    return np.exp2(a.ravel()).repeat(32)


def f64(x):
    return np.asarray(x).astype(np.float64)


def striped(idx):
    return np.tile(idx.reshape(-1, 16).T, (8, 1)).astype(np.uint16)


def unstriped(offs):
    return offs[:16].T.reshape(-1).astype(np.int64)


def pack_weight(w):
    k, n = w.shape
    w = f64(np.asarray(w, np.float32).astype(ml_dtypes.bfloat16)).reshape(k // 32, 32, n)
    amax = np.abs(w).max(1)
    byte = np.clip(np.where(amax > 0, np.frexp(amax)[1] - 1 + 127 - 7, 1), 1, 254)
    scaled = (w * np.exp2(127.0 - byte)[:, None, :]).reshape(k, n).astype(np.float32)
    words = np.ascontiguousarray(scaled.reshape(k // 512, 128, 4, n).transpose(0, 1, 3, 2)).astype(ml_dtypes.float8_e4m3fn).view(np.uint8)
    return words, np.ascontiguousarray(byte.astype(np.uint8).reshape(k // 512, 16, n))


def unpack_weight(words, scales):
    g, p, n, _ = words.shape
    vals = np.ascontiguousarray(words).view(ml_dtypes.float8_e4m3fn).astype(np.float64) * np.repeat(np.exp2(scales.astype(np.float64) - 127.0), 8, axis=1)[..., None]
    return vals.transpose(0, 1, 3, 2).reshape(g * 512, n)


K, T, S, N, H, U = 512, 2048, 512, 256, 512, 1024


def setup_inputs():
    n = np.random.standard_normal
    s = mx_kscale(K)[:, None]
    u = mx_kscale(H)
    packed_xT = pack_weight(n((K, T)) * s)
    return {
        "x_words": packed_xT[0],
        "x_scales": packed_xT[1],
        "w1": (n((K, H)) / np.sqrt(K) / s).astype(np.float32),
        "unit": (np.random.uniform(0.6, 1.4, (H, 1)) * u[:, None]).astype(np.float32),
        "w2": (n((H, N)) / np.sqrt(H) / u[:, None]).astype(np.float32),
        "offs": striped(np.random.permutation(T)[:S]),
        "rw_": striped(np.random.permutation(np.concatenate([np.arange(S), np.random.randint(0, S, U - S)]))),
        "cl": striped(np.random.permutation(np.concatenate([np.arange(S), np.random.randint(0, S, U - S)]))),
        "dg": striped(np.random.permutation(np.concatenate([np.arange(S), np.random.randint(0, S, U - S)]))),
    }


def reference(x_words, x_scales, w1, unit, w2, offs, rw_, cl, dg):
    xq = unpack_weight(x_words, x_scales)[:, unstriped(offs)]
    y = mxq(f64(w1), 0, "e4m3").T @ xq
    yr = y[:, unstriped(rw_)]
    yc2 = y[:, unstriped(cl)]
    prd = yr * yc2
    mx2 = np.maximum(yr, yc2)
    yd_ = y[:, unstriped(dg)]
    hid = f64(unit) * (prd - mx2 + yd_)
    return mxq(f64(w2), 0, "e4m3").T @ mxq(hid, 0, "e4m3")

@@ -1,0 +1,211 @@
+from contextlib import ExitStack
+
+import concourse.mybir as mybir
+
+K, T, S, N, H, U = 512, 2048, 512, 256, 512, 1024
+FLOPS = 2 * K * H * S + 2 * H * N * U
+
+F32 = mybir.dt.float32
+BF16 = mybir.dt.bfloat16
+I32 = mybir.dt.int32
+U32 = mybir.dt.uint32
+U16 = mybir.dt.uint16
+U8 = mybir.dt.uint8
+FP8X4 = mybir.dt.float8_e4m3fn_x4
+ALU = mybir.AluOpType
+COPY = mybir.ActivationFunctionType.Copy
+
+P = 128
+PACK = 4
+LIST_ROWS = 16
+RUN = 4
+WIDE = 2 * S
+NARROW = S + 64
+CHUNKS = [512,384,128]
+FUSED_UNITS = 4
+RING = 3
+
+
+def tile_picked_yrowcol_upd_p_kernel(
+    tc, x_words, x_scales, w1, unit, w2, offs, rw_, cl, dg, out
+):
+    nc = tc.nc
+    with ExitStack() as ctx:
+        keep = ctx.enter_context(tc.tile_pool(name="keep", bufs=1))
+        ring = ctx.enter_context(tc.tile_pool(name="ring", bufs=RING))
+        psum_y = ctx.enter_context(tc.psum_pool(name="psum_y", bufs=1))
+        psum_out = ctx.enter_context(tc.psum_pool(name="psum_out", bufs=2))
+
+        offs_sb = keep.tile([P, S // LIST_ROWS], U16, name="offs_sb")
+        row_sb = keep.tile([P, U // LIST_ROWS], U16, name="row_sb")
+        col_sb = keep.tile([P, U // LIST_ROWS], U16, name="col_sb")
+        diag_sb = keep.tile([P, U // LIST_ROWS], U16, name="diag_sb")
+
+        table_words = keep.tile([P, T], U32, name="table_words", align_bytes=64)
+        table_scales = keep.tile([P, T], U8, name="table_scales", align_bytes=64)
+        half = H // 2
+        w1_raw = [keep.tile([P, PACK, half], F32, name=f"w1_raw{s}") for s in range(2)]
+        w2_raw = keep.tile([P, PACK, N], F32, name="w2_raw")
+        unit_sb = keep.tile([P, PACK], F32, name="unit_sb")
+
+        nc.sync.dma_start(out=offs_sb[:], in_=offs)
+        nc.sync.dma_start(
+            out=table_words[:].bitcast(I32), in_=x_words[0].rearrange("p c r -> p (c r)").bitcast(I32)
+        )
+        nc.vector.memset(table_scales[:].bitcast(I32), 0)
+        for q in range(4):
+            nc.scalar.dma_start(
+                out=table_scales[32 * q : 32 * q + 4, :].bitcast(I32),
+                in_=x_scales[0, 4 * q : 4 * q + 4, :].bitcast(I32),
+            )
+        w1_rows = w1.rearrange("(p j) c -> p j c", j=PACK)
+        for s in range(2):
+            nc.sync.dma_start(out=w1_raw[s][:], in_=w1_rows[:, :, s * half : (s + 1) * half])
+        nc.sync.dma_start(out=unit_sb[:], in_=unit.rearrange("(p t) o -> p (t o)", t=PACK))
+        nc.sync.dma_start(out=col_sb[:], in_=cl)
+        nc.sync.dma_start(out=row_sb[:], in_=rw_)
+        nc.sync.dma_start(out=diag_sb[:], in_=dg)
+        nc.sync.dma_start(out=w2_raw[:], in_=w2.rearrange("(p j) c -> p j c", j=PACK))
+
+        y = [keep.tile([P, NARROW], F32, name=f"y{t}") for t in range(PACK)]
+        z = [keep.tile([P, WIDE], F32, name=f"z{t}") for t in range(PACK)]
+        for plane in y + z:
+            nc.vector.memset(plane[:, S:], 0.0)
+
+        half_sign = keep.tile([P, PACK], F32, name="half_sign")
+        unit_sign = keep.tile([P, PACK], F32, name="unit_sign")
+        unit_size = keep.tile([P, PACK], F32, name="unit_size")
+        nc.gpsimd.tensor_scalar(half_sign[:], unit_sb[:], 0.0, 0.5, ALU.is_ge, ALU.subtract)
+        nc.gpsimd.tensor_scalar(unit_sign[:], half_sign[:], 2.0, 0.0, ALU.mult, ALU.add)
+        nc.gpsimd.tensor_tensor(unit_size[:], unit_sb[:], unit_sign[:], ALU.mult)
+
+        x_codes = keep.tile([P, S], U32, name="x_codes", align_bytes=64)
+        x_bytes = keep.tile([P, S], U8, name="x_bytes", align_bytes=64)
+        nc.vector.tensor_copy(out=x_bytes[:], in_=table_scales[:].indirect(offs_sb[:]))
+        nc.vector.tensor_copy(out=x_codes[:], in_=table_words[:].indirect(offs_sb[:]))
+
+        m_half = P // 2
+        w1_codes = keep.tile([P, PACK, P], U32, name="w1_codes", align_bytes=64)
+        w1_bytes = keep.tile([P, PACK, P], U8, name="w1_bytes", align_bytes=64)
+        for s in range(2):
+            grouped = keep.tile([P, PACK, m_half, PACK], BF16, name=f"w1_grouped{s}", align_bytes=64)
+            dst = grouped[:].rearrange("p t m j -> p m t j")
+            src = w1_raw[s][:].rearrange("p j (m t) -> p m t j", t=PACK)
+            if s == 0:
+                nc.scalar.activation(dst, src, COPY)
+            else:
+                nc.vector.tensor_copy(out=dst, in_=src)
+            cols = slice(s * m_half, (s + 1) * m_half)
+            for t in range(PACK):
+                nc.vector.quantize_mx(
+                    out=w1_codes[:, t, cols].bitcast(FP8X4),
+                    scales=w1_bytes[:, t, cols],
+                    in_=grouped[:, t].rearrange("p m j -> p (m j)"),
+                )
+
+        for t in range(PACK):
+            bank = psum_y.tile([P, S], F32, name=f"y_bank{t}")
+            nc.tensor.matmul_mx(
+                out=bank[:],
+                lhsT=w1_codes[:, t, :].bitcast(FP8X4),
+                lhsT_scale=w1_bytes[:, t, :],
+                rhs=x_codes[:].bitcast(FP8X4),
+                rhs_scale=x_bytes[:],
+                start=True,
+                stop=True,
+            )
+            if t in [0,1,2,3]:
+                nc.scalar.copy(out=y[t][:, :S], in_=bank[:])
+            else:
+                nc.vector.tensor_copy(out=y[t][:, :S], in_=bank[:])
+            nc.vector.tensor_scalar(z[t][:, :S], y[t][:, :S], unit_size[:, t : t + 1], None, ALU.mult)
+
+        w2_grouped = keep.tile([P, N, PACK], BF16, name="w2_grouped", align_bytes=64)
+        nc.vector.tensor_tensor(
+            w2_grouped[:].rearrange("p (c i) j -> p c j i", i=RUN),
+            w2_raw[:].rearrange("p j (c i) -> p c j i", i=RUN),
+            unit_sign[:].unsqueeze(1).unsqueeze(3).to_broadcast([P, N // RUN, PACK, RUN]),
+            ALU.mult,
+        )
+        w2_codes = keep.tile([P, N], U32, name="w2_codes", align_bytes=64)
+        w2_bytes = keep.tile([P, N], U8, name="w2_bytes", align_bytes=64)
+        nc.vector.quantize_mx(
+            out=w2_codes[:].bitcast(FP8X4), scales=w2_bytes[:], in_=w2_grouped[:].rearrange("p c j -> p (c j)")
+        )
+
+        out_rows = out.rearrange("(h p) r -> p h r", p=P)
+        widest = max(CHUNKS)
+
+        def join(index, n, product, rest):
+            grouped = keep.tile([P, n, PACK], BF16, name=f"hid_grouped{index}", align_bytes=64)
+            nc.vector.tensor_tensor(
+                grouped[:].rearrange("p (c i) t -> p c t i", i=RUN),
+                product[:].rearrange("p t (c i) -> p c t i", i=RUN),
+                rest[:].rearrange("p t (c i) -> p c t i", i=RUN),
+                ALU.add,
+            )
+            return grouped
+
+        def finish(index, r0, n, grouped):
+            codes = keep.tile([P, n], U32, name=f"hid_codes{index}", align_bytes=64)
+            scale_bytes = keep.tile([P, n], U8, name=f"hid_bytes{index}", align_bytes=64)
+            nc.vector.quantize_mx(
+                out=codes[:].bitcast(FP8X4), scales=scale_bytes[:], in_=grouped[:].rearrange("p c t -> p (c t)")
+            )
+            result = keep.tile([P, 2, n], F32, name=f"result{index}")
+            pieces = [slice(0, 256), slice(256, n)] if n == 384 else [slice(0, n)]
+            for h in range(2):
+                bank = psum_out.tile([P, widest], F32, name=f"out_bank{h}")
+                for cols in pieces:
+                    nc.tensor.matmul_mx(
+                        out=bank[:, cols],
+                        lhsT=w2_codes[:, h * P : (h + 1) * P].bitcast(FP8X4),
+                        lhsT_scale=w2_bytes[:, h * P : (h + 1) * P],
+                        rhs=codes[:, cols].bitcast(FP8X4),
+                        rhs_scale=scale_bytes[:, cols],
+                        start=True,
+                        stop=True,
+                    )
+                if index == len(CHUNKS) - 1 and h == 1:
+                    nc.vector.tensor_copy(out=result[:, h, :], in_=bank[:, :n])
+                else:
+                    nc.scalar.copy(out=result[:, h, :], in_=bank[:, :n])
+            nc.sync.dma_start(out=out_rows[:, :, r0 : r0 + n], in_=result[:])
+
+        waiting = []
+        r0 = 0
+        for index, n in enumerate(CHUNKS):
+            entries = slice(r0 // LIST_ROWS, (r0 + n) // LIST_ROWS)
+            product = keep.tile([P, PACK, n], F32, name=f"product{index}")
+            rest = keep.tile([P, PACK, n], F32, name=f"rest{index}")
+            for t in range(PACK):
+                step = index * PACK + t
+                a = ring.tile([P, widest], F32, name="a")
+                b = ring.tile([P, widest], F32, name="b")
+                larger = ring.tile([P, widest], F32, name="larger")
+                nc.scalar.activation(b[:, :n], y[t][:].indirect(col_sb[:, entries]), COPY)
+                if step in [0]:
+                    nc.vector.tensor_copy(out=a[:, :n], in_=z[t][:].indirect(row_sb[:, entries]))
+                else:
+                    nc.scalar.activation(a[:, :n], z[t][:].indirect(row_sb[:, entries]), COPY)
+                diagonal = z[t][:].indirect(diag_sb[:, entries])
+                if step >= FUSED_UNITS:
+                    d = ring.tile([P, widest], F32, name="d")
+                    nc.scalar.activation(d[:, :n], diagonal, COPY)
+                    diagonal = d[:, :n]
+                nc.vector.scalar_tensor_tensor(
+                    larger[:, :n], b[:, :n], unit_size[:, t : t + 1], a[:, :n], ALU.mult, ALU.max
+                )
+                nc.vector.tensor_tensor(product[:, t, :], a[:, :n], b[:, :n], ALU.mult)
+                if waiting:
+                    waiting.pop(0)()
+                nc.vector.tensor_tensor(rest[:, t, :], diagonal, larger[:, :n], ALU.subtract)
+
+            def first(index=index, r0=r0, n=n, product=product, rest=rest):
+                grouped = join(index, n, product, rest)
+                waiting.append(lambda: finish(index, r0, n, grouped))
+
+            waiting.append(first)
+            r0 = r0 + n
+        waiting.pop(0)()
+        waiting.pop(0)()

@@ -54,7 +54,7 @@ def tile_picked_yrowcol_upd_p_kernel(
         )
         nc.vector.memset(table_scales[:].bitcast(I32), 0)
         for q in range(4):
-            nc.scalar.dma_start(
+            nc.sync.dma_start(
                 out=table_scales[32 * q : 32 * q + 4, :].bitcast(I32),
                 in_=x_scales[0, 4 * q : 4 * q + 4, :].bitcast(I32),
             )
@@ -94,7 +94,8 @@ def tile_picked_yrowcol_upd_p_kernel(
             if s == 0:
                 nc.scalar.activation(dst, src, COPY)
             else:
-                nc.vector.tensor_copy(out=dst, in_=src)
+                nc.scalar.activation(dst[:, :24], src[:, :24], COPY)
+                nc.vector.tensor_copy(out=dst[:, 24:], in_=src[:, 24:])
             cols = slice(s * m_half, (s + 1) * m_half)
             for t in range(PACK):
                 nc.vector.quantize_mx(

from contextlib import ExitStack

import concourse.mybir as mybir

K, T, S, N, H, U = 512, 2048, 512, 256, 512, 1024
FLOPS = 2 * K * H * S + 2 * H * N * U

F32 = mybir.dt.float32
BF16 = mybir.dt.bfloat16
I32 = mybir.dt.int32
U32 = mybir.dt.uint32
U16 = mybir.dt.uint16
U8 = mybir.dt.uint8
FP8X4 = mybir.dt.float8_e4m3fn_x4
ALU = mybir.AluOpType
COPY = mybir.ActivationFunctionType.Copy

P = 128
PACK = 4
LIST_ROWS = 16
RUN = 4
WIDE = 2 * S
NARROW = S + 64
CHUNKS = [512,384,128]
FUSED_UNITS = 4
RING = 3


def tile_picked_yrowcol_upd_p_kernel(
    tc, x_words, x_scales, w1, unit, w2, offs, rw_, cl, dg, out
):
    nc = tc.nc
    with ExitStack() as ctx:
        keep = ctx.enter_context(tc.tile_pool(name="keep", bufs=1))
        ring = ctx.enter_context(tc.tile_pool(name="ring", bufs=RING))
        psum_y = ctx.enter_context(tc.psum_pool(name="psum_y", bufs=1))
        psum_out = ctx.enter_context(tc.psum_pool(name="psum_out", bufs=2))

        offs_sb = keep.tile([P, S // LIST_ROWS], U16, name="offs_sb")
        row_sb = keep.tile([P, U // LIST_ROWS], U16, name="row_sb")
        col_sb = keep.tile([P, U // LIST_ROWS], U16, name="col_sb")
        diag_sb = keep.tile([P, U // LIST_ROWS], U16, name="diag_sb")

        table_words = keep.tile([P, T], U32, name="table_words", align_bytes=64)
        table_scales = keep.tile([P, T], U8, name="table_scales", align_bytes=64)
        half = H // 2
        w1_raw = [keep.tile([P, PACK, half], F32, name=f"w1_raw{s}") for s in range(2)]
        w2_raw = keep.tile([P, PACK, N], F32, name="w2_raw")
        unit_sb = keep.tile([P, PACK], F32, name="unit_sb")

        nc.sync.dma_start(out=offs_sb[:], in_=offs)
        nc.sync.dma_start(
            out=table_words[:].bitcast(I32), in_=x_words[0].rearrange("p c r -> p (c r)").bitcast(I32)
        )
        nc.vector.memset(table_scales[:].bitcast(I32), 0)
        for q in range(4):
            nc.sync.dma_start(
                out=table_scales[32 * q : 32 * q + 4, :].bitcast(I32),
                in_=x_scales[0, 4 * q : 4 * q + 4, :].bitcast(I32),
            )
        w1_rows = w1.rearrange("(p j) c -> p j c", j=PACK)
        for s in range(2):
            nc.sync.dma_start(out=w1_raw[s][:], in_=w1_rows[:, :, s * half : (s + 1) * half])
        nc.sync.dma_start(out=unit_sb[:], in_=unit.rearrange("(p t) o -> p (t o)", t=PACK))
        nc.sync.dma_start(out=col_sb[:], in_=cl)
        nc.sync.dma_start(out=row_sb[:], in_=rw_)
        nc.sync.dma_start(out=diag_sb[:], in_=dg)
        nc.sync.dma_start(out=w2_raw[:], in_=w2.rearrange("(p j) c -> p j c", j=PACK))

        y = [keep.tile([P, NARROW], F32, name=f"y{t}") for t in range(PACK)]
        z = [keep.tile([P, WIDE], F32, name=f"z{t}") for t in range(PACK)]
        for plane in y + z:
            nc.vector.memset(plane[:, S:], 0.0)

        half_sign = keep.tile([P, PACK], F32, name="half_sign")
        unit_sign = keep.tile([P, PACK], F32, name="unit_sign")
        unit_size = keep.tile([P, PACK], F32, name="unit_size")
        nc.gpsimd.tensor_scalar(half_sign[:], unit_sb[:], 0.0, 0.5, ALU.is_ge, ALU.subtract)
        nc.gpsimd.tensor_scalar(unit_sign[:], half_sign[:], 2.0, 0.0, ALU.mult, ALU.add)
        nc.gpsimd.tensor_tensor(unit_size[:], unit_sb[:], unit_sign[:], ALU.mult)

        x_codes = keep.tile([P, S], U32, name="x_codes", align_bytes=64)
        x_bytes = keep.tile([P, S], U8, name="x_bytes", align_bytes=64)
        nc.vector.tensor_copy(out=x_bytes[:], in_=table_scales[:].indirect(offs_sb[:]))
        nc.vector.tensor_copy(out=x_codes[:], in_=table_words[:].indirect(offs_sb[:]))

        m_half = P // 2
        w1_codes = keep.tile([P, PACK, P], U32, name="w1_codes", align_bytes=64)
        w1_bytes = keep.tile([P, PACK, P], U8, name="w1_bytes", align_bytes=64)
        for s in range(2):
            grouped = keep.tile([P, PACK, m_half, PACK], BF16, name=f"w1_grouped{s}", align_bytes=64)
            dst = grouped[:].rearrange("p t m j -> p m t j")
            src = w1_raw[s][:].rearrange("p j (m t) -> p m t j", t=PACK)
            if s == 0:
                nc.scalar.activation(dst, src, COPY)
            else:
                nc.scalar.activation(dst[:, :24], src[:, :24], COPY)
                nc.vector.tensor_copy(out=dst[:, 24:], in_=src[:, 24:])
            cols = slice(s * m_half, (s + 1) * m_half)
            for t in range(PACK):
                nc.vector.quantize_mx(
                    out=w1_codes[:, t, cols].bitcast(FP8X4),
                    scales=w1_bytes[:, t, cols],
                    in_=grouped[:, t].rearrange("p m j -> p (m j)"),
                )

        for t in range(PACK):
            bank = psum_y.tile([P, S], F32, name=f"y_bank{t}")
            nc.tensor.matmul_mx(
                out=bank[:],
                lhsT=w1_codes[:, t, :].bitcast(FP8X4),
                lhsT_scale=w1_bytes[:, t, :],
                rhs=x_codes[:].bitcast(FP8X4),
                rhs_scale=x_bytes[:],
                start=True,
                stop=True,
            )
            if t in [0,1,2,3]:
                nc.scalar.copy(out=y[t][:, :S], in_=bank[:])
            else:
                nc.vector.tensor_copy(out=y[t][:, :S], in_=bank[:])
            nc.vector.tensor_scalar(z[t][:, :S], y[t][:, :S], unit_size[:, t : t + 1], None, ALU.mult)

        w2_grouped = keep.tile([P, N, PACK], BF16, name="w2_grouped", align_bytes=64)
        nc.vector.tensor_tensor(
            w2_grouped[:].rearrange("p (c i) j -> p c j i", i=RUN),
            w2_raw[:].rearrange("p j (c i) -> p c j i", i=RUN),
            unit_sign[:].unsqueeze(1).unsqueeze(3).to_broadcast([P, N // RUN, PACK, RUN]),
            ALU.mult,
        )
        w2_codes = keep.tile([P, N], U32, name="w2_codes", align_bytes=64)
        w2_bytes = keep.tile([P, N], U8, name="w2_bytes", align_bytes=64)
        nc.vector.quantize_mx(
            out=w2_codes[:].bitcast(FP8X4), scales=w2_bytes[:], in_=w2_grouped[:].rearrange("p c j -> p (c j)")
        )

        out_rows = out.rearrange("(h p) r -> p h r", p=P)
        widest = max(CHUNKS)

        def join(index, n, product, rest):
            grouped = keep.tile([P, n, PACK], BF16, name=f"hid_grouped{index}", align_bytes=64)
            nc.vector.tensor_tensor(
                grouped[:].rearrange("p (c i) t -> p c t i", i=RUN),
                product[:].rearrange("p t (c i) -> p c t i", i=RUN),
                rest[:].rearrange("p t (c i) -> p c t i", i=RUN),
                ALU.add,
            )
            return grouped

        def finish(index, r0, n, grouped):
            codes = keep.tile([P, n], U32, name=f"hid_codes{index}", align_bytes=64)
            scale_bytes = keep.tile([P, n], U8, name=f"hid_bytes{index}", align_bytes=64)
            nc.vector.quantize_mx(
                out=codes[:].bitcast(FP8X4), scales=scale_bytes[:], in_=grouped[:].rearrange("p c t -> p (c t)")
            )
            result = keep.tile([P, 2, n], F32, name=f"result{index}")
            pieces = [slice(0, 256), slice(256, n)] if n == 384 else [slice(0, n)]
            for h in range(2):
                bank = psum_out.tile([P, widest], F32, name=f"out_bank{h}")
                for cols in pieces:
                    nc.tensor.matmul_mx(
                        out=bank[:, cols],
                        lhsT=w2_codes[:, h * P : (h + 1) * P].bitcast(FP8X4),
                        lhsT_scale=w2_bytes[:, h * P : (h + 1) * P],
                        rhs=codes[:, cols].bitcast(FP8X4),
                        rhs_scale=scale_bytes[:, cols],
                        start=True,
                        stop=True,
                    )
                if index == len(CHUNKS) - 1 and h == 1:
                    nc.vector.tensor_copy(out=result[:, h, :], in_=bank[:, :n])
                else:
                    nc.scalar.copy(out=result[:, h, :], in_=bank[:, :n])
            nc.sync.dma_start(out=out_rows[:, :, r0 : r0 + n], in_=result[:])

        waiting = []
        r0 = 0
        for index, n in enumerate(CHUNKS):
            entries = slice(r0 // LIST_ROWS, (r0 + n) // LIST_ROWS)
            product = keep.tile([P, PACK, n], F32, name=f"product{index}")
            rest = keep.tile([P, PACK, n], F32, name=f"rest{index}")
            for t in range(PACK):
                step = index * PACK + t
                a = ring.tile([P, widest], F32, name="a")
                b = ring.tile([P, widest], F32, name="b")
                larger = ring.tile([P, widest], F32, name="larger")
                nc.scalar.activation(b[:, :n], y[t][:].indirect(col_sb[:, entries]), COPY)
                if step in [0]:
                    nc.vector.tensor_copy(out=a[:, :n], in_=z[t][:].indirect(row_sb[:, entries]))
                else:
                    nc.scalar.activation(a[:, :n], z[t][:].indirect(row_sb[:, entries]), COPY)
                diagonal = z[t][:].indirect(diag_sb[:, entries])
                if step >= FUSED_UNITS:
                    d = ring.tile([P, widest], F32, name="d")
                    nc.scalar.activation(d[:, :n], diagonal, COPY)
                    diagonal = d[:, :n]
                nc.vector.scalar_tensor_tensor(
                    larger[:, :n], b[:, :n], unit_size[:, t : t + 1], a[:, :n], ALU.mult, ALU.max
                )
                nc.vector.tensor_tensor(product[:, t, :], a[:, :n], b[:, :n], ALU.mult)
                if waiting:
                    waiting.pop(0)()
                nc.vector.tensor_tensor(rest[:, t, :], diagonal, larger[:, :n], ALU.subtract)

            def first(index=index, r0=r0, n=n, product=product, rest=rest):
                grouped = join(index, n, product, rest)
                waiting.append(lambda: finish(index, r0, n, grouped))

            waiting.append(first)
            r0 = r0 + n
        waiting.pop(0)()
        waiting.pop(0)()
